import numpy as np
import ml_dtypes


def mxq(x, axis, fmt="e4m3"):
    dtype, down = {"e4m3": (ml_dtypes.float8_e4m3fn, 7), "e5m2": (ml_dtypes.float8_e5m2, 14)}[fmt]
    v = np.moveaxis(np.asarray(x, np.float32).astype(ml_dtypes.bfloat16).astype(np.float64), axis, -1)
    blocks = v.reshape(v.shape[:-1] + (-1, 32))
    amax = np.abs(blocks).max(-1, keepdims=True)
    byte = np.maximum(np.where(amax > 0, np.frexp(amax)[1] - 1 + 127, 0) - down, 1)
    scale = np.exp2(byte - 127.0)
    codes = (blocks / scale).astype(np.float32).astype(dtype).astype(np.float64)
    return np.moveaxis((codes * scale).reshape(v.shape), -1, axis)


WIDE = False


def mx_kscale(k):
    if not WIDE:
        return np.ones(k)
    levels = np.array([10, -10, 5, -5, 0])
    if k % 512:
        return np.exp2(np.random.permutation(np.resize(levels, k // 32))).repeat(32)
    a = np.empty((k // 512, 16))
    for p in range(k // 512):
        a[p, :8] = np.random.permutation(np.resize(levels, 8))
        for g in range(8):
            far = levels[np.abs(levels - a[p, g]) >= 10]
            a[p, g + 8] = far[np.random.randint(len(far))]
    return np.exp2(a.ravel()).repeat(32)


def f64(x):
    return np.asarray(x).astype(np.float64)


def striped(idx):
    return np.tile(idx.reshape(-1, 16).T, (8, 1)).astype(np.uint16)


def unstriped(offs):
    return offs[:16].T.reshape(-1).astype(np.int64)


E2M1 = np.array([0.0, 0.5, 1.0, 1.5, 2.0, 3.0, 4.0, 6.0, -0.0, -0.5, -1.0, -1.5, -2.0, -3.0, -4.0, -6.0])


def pack_weight(w, fmt):
    k, n = w.shape
    w = f64(np.asarray(w, np.float32).astype(ml_dtypes.bfloat16)).reshape(k // 32, 32, n)
    amax = np.abs(w).max(1)
    if fmt == "e4m3":
        byte = np.frexp(amax)[1] - 1 + 127 - 7
    else:
        mant, ex = np.frexp(amax / 6.0)
        byte = np.where(mant > 0.5, ex, ex - 1) + 127
    byte = np.clip(np.where(amax > 0, byte, 1), 1, 254)
    scaled = (w * np.exp2(127.0 - byte)[:, None, :]).reshape(k, n).astype(np.float32)
    by_word = np.ascontiguousarray(scaled.reshape(k // 512, 128, 4, n).transpose(0, 1, 3, 2))
    if fmt == "e4m3":
        words = by_word.astype(ml_dtypes.float8_e4m3fn).view(np.uint8)
    else:
        c = by_word.astype(ml_dtypes.float4_e2m1fn).view(np.uint8) & 0xF
        words = (c[..., 0::2] | (c[..., 1::2] << 4)).reshape(k // 512, 128, 2 * n)
    return np.ascontiguousarray(words), np.ascontiguousarray(byte.astype(np.uint8).reshape(k // 512, 16, n))


def unpack_weight(words, scales, fmt):
    g, _, n = scales.shape
    words = np.ascontiguousarray(words).reshape(g, 128, n, -1)
    if fmt == "e4m3":
        vals = words.view(ml_dtypes.float8_e4m3fn).astype(np.float64)
    else:
        nib = np.empty((g, 128, n, 4), np.uint8)
        nib[..., 0::2] = words & 0xF
        nib[..., 1::2] = words >> 4
        vals = E2M1[nib]
    vals = vals * np.repeat(np.exp2(scales.astype(np.float64) - 127.0), 8, axis=1)[..., None]
    return vals.transpose(0, 1, 3, 2).reshape(g * 512, n)


def gelu(v):
    return 0.5 * v * (1.0 + np.tanh(np.sqrt(2.0 / np.pi) * (v + 0.044715 * v**3)))


K, T, E, C, H, N = 512, 512, 4, 128, 1024, 128


def by_expert(wq, xq):
    return np.concatenate([wq[e].T @ xq[:, e * C:(e + 1) * C] for e in range(E)], axis=1)


def setup_inputs():
    n = np.random.standard_normal
    s = mx_kscale(K)[:, None]
    u = mx_kscale(H)
    w1 = [pack_weight(m, "e2m1") for m in n((E + 1, K, H)) / np.sqrt(K) / s[None]]
    w3 = [pack_weight(m, "e2m1") for m in n((E + 1, K, H)) / np.sqrt(K) / s[None] * u[None, None, :]]
    w2 = [pack_weight(m, "e2m1") for m in n((E + 1, H, N)) / np.sqrt(H) / u[None, :, None]]
    x = pack_weight(n((K, T)) * s, "e4m3")
    return {
        "x_words": x[0],
        "x_scales": x[1],
        "w1_words": np.stack([m[0] for m in w1]),
        "w1_scales": np.stack([m[1] for m in w1]),
        "w3_words": np.stack([m[0] for m in w3]),
        "w3_scales": np.stack([m[1] for m in w3]),
        "w2_words": np.stack([m[0] for m in w2]),
        "w2_scales": np.stack([m[1] for m in w2]),
        "gate": np.tile(np.random.uniform(0.2, 1.0, E * C), (N, 1)).astype(np.float32),
        "offs": striped(np.random.permutation(T)[:E * C]),
    }


def reference(x_words, x_scales, w1_words, w1_scales, w3_words, w3_scales, w2_words, w2_scales, gate, offs):
    idx = unstriped(offs)
    w1 = np.stack([unpack_weight(w1_words[e], w1_scales[e], "e2m1") for e in range(E + 1)])
    w3 = np.stack([unpack_weight(w3_words[e], w3_scales[e], "e2m1") for e in range(E + 1)])
    w2 = np.stack([unpack_weight(w2_words[e], w2_scales[e], "e2m1") for e in range(E + 1)])
    w1q, w3q, w2q = w1, w3, w2
    xs = unpack_weight(x_words, x_scales, "e4m3")
    hs = gelu(w1q[E].T @ xs) * (w3q[E].T @ xs)
    ys = w2q[E].T @ mxq(hs, 0, "e4m3")
    xq = unpack_weight(x_words, x_scales, "e4m3")[:, idx]
    h = gelu(by_expert(w1q, xq))
    h = h * by_expert(w3q, xq)
    y = by_expert(w2q, mxq(h, 0, "e4m3"))
    out = ys
    out[:, idx] += f64(gate) * y
    return out

@@ -1,0 +1,232 @@
+from contextlib import ExitStack
+
+import concourse.mybir as mybir
+from concourse.masks import make_identity
+
+K, T, E, C, H, N = 512, 512, 4, 128, 1024, 128
+FLOPS = 2 * (E * C + T) * (2 * K * H + H * N)
+
+F32 = mybir.dt.float32
+BF16 = mybir.dt.bfloat16
+I32 = mybir.dt.int32
+U32 = mybir.dt.uint32
+U16 = mybir.dt.uint16
+U8 = mybir.dt.uint8
+FP8X4 = mybir.dt.float8_e4m3fn_x4
+FP4X4 = mybir.dt.float4_e2m1fn_x4
+GELU = mybir.ActivationFunctionType.Gelu_apprx_tanh
+MULT = mybir.AluOpType.mult
+ADD = mybir.AluOpType.add
+
+P = 128
+PASS = 512
+S = H // PASS
+SHARED = E
+GATHER = 256
+
+
+def load_scale_rows(queue, plane, rows, which=range(4)):
+    by_r = rows.rearrange("(q r) w -> r q w" if rows.ndim == 2 else "(q r) m w -> r q m w", r=4)
+    for r in which:
+        place = plane[r:P:32, :].bitcast(I32)
+        if rows.ndim == 3:
+            place = place.rearrange("q (m w) -> q m w", m=rows.shape[1])
+        queue.dma_start(out=place, in_=by_r[r].bitcast(I32))
+
+
+def tile_moe_shr_glu_gelu_kernel(
+    tc, x_words, x_scales, w1_words, w1_scales, w3_words, w3_scales, w2_words, w2_scales, gate, offs, out
+):
+    nc = tc.nc
+    with ExitStack() as ctx:
+        keep = ctx.enter_context(tc.tile_pool(name="keep", bufs=1))
+        psum = ctx.enter_context(tc.psum_pool(name="psum", bufs=1))
+
+        def tiles(name, count, shape, dtype):
+            return [keep.tile(shape, dtype, name=f"{name}{j}", align_bytes=64) for j in range(count)]
+
+        steps = [(SHARED, 0), (SHARED, 1)] + [(e, e) for e in range(E)] + [(SHARED, 2), (SHARED, 3)]
+        n = len(steps)
+
+        offsets = keep.tile([P, T // 16], U16, name="offsets")
+        xw = keep.tile([P, T], U32, name="xw", align_bytes=64)
+        xs = keep.tile([P, T], U8, name="xs", align_bytes=64)
+        w1_sh = keep.tile([P, 3 * H], U8, name="w1_sh", align_bytes=64)
+        w3_sh = keep.tile([P, 3 * H], U8, name="w3_sh", align_bytes=64)
+        w1s_sh, w1w_sh = w1_sh[:, :H], w1_sh[:, H:]
+        w3s_sh, w3w_sh = w3_sh[:, :H], w3_sh[:, H:]
+        w1_ro = keep.tile([P, 3 * E * H], U8, name="w1_ro", align_bytes=64)
+        w3_ro = keep.tile([P, 3 * E * H], U8, name="w3_ro", align_bytes=64)
+        w1s_ro = w1_ro[:, E * H : 2 * E * H]
+        w3s_ro = w3_ro[:, E * H : 2 * E * H]
+        w1w_ro = (w1_ro[:, : E * H], w1_ro[:, 2 * E * H :])
+        w3w_ro = (w3_ro[:, : E * H], w3_ro[:, 2 * E * H :])
+        w2_cols = (E + 1) * S * N
+        w2_sb = keep.tile([P, 3 * w2_cols], U8, name="w2_sb", align_bytes=64)
+        w2w = w2_sb[:, : 2 * w2_cols]
+        w2s = w2_sb[:, 2 * w2_cols :]
+        w1w = [w1w_ro[e // 2][:, 2 * H * (e % 2) : 2 * H * (e % 2 + 1)] for e in range(E)] + [w1w_sh]
+        w3w = [w3w_ro[e // 2][:, 2 * H * (e % 2) : 2 * H * (e % 2 + 1)] for e in range(E)] + [w3w_sh]
+        gate_sb = keep.tile([P, E * C], F32, name="gate_sb")
+        ident = keep.tile([P, P], F32, name="ident")
+        routed = keep.tile([P, T], F32, name="routed")
+        gw = tiles("gw", T // GATHER, [P, GATHER], U32)
+        gs = tiles("gs", T // GATHER, [P, GATHER], U8)
+        g_ring = tiles("g", 4, [P, PASS], F32)
+        h_all = tiles("h", n, [P, H], BF16)
+        ht_all = tiles("ht", n, [P, S * C * 4], BF16)
+        hq_all = tiles("hq", n, [P, S * C], U32)
+        hs_all = tiles("hs", n, [P, S * C], U8)
+        y_all = tiles("y", E, [P, C], F32)
+        early = keep.tile([P, 3 * C], F32, name="early")
+        last = keep.tile([P, C], F32, name="last")
+        a_banks = [psum.tile([P, PASS], F32, name=f"a_bank{j}") for j in range(4)]
+        b_banks = [psum.tile([P, PASS], F32, name=f"b_bank{j}") for j in range(3)]
+        y_bank = psum.tile([P, T], F32, name="y_bank")
+
+        for plane in (
+            xs[:],
+            w1_sh[:, : H + 32],
+            w3_sh[:, : H + 32],
+            w1_ro[:, E * H - 32 : 2 * E * H + 32],
+            w3_ro[:, E * H - 32 : 2 * E * H + 32],
+            w2_sb[:, 2 * w2_cols - 32 :],
+        ):
+            nc.vector.memset(plane.bitcast(I32), 0)
+        make_identity(nc, ident[:])
+
+        def load_words(tile, words):
+            nc.sync.dma_start(
+                out=tile.bitcast(I32).rearrange("p (m w) -> p m w", m=words.shape[0] * words.shape[1]),
+                in_=words.rearrange("e s p n -> p (e s) n").bitcast(I32),
+            )
+
+        ro1 = w1_scales[0:E].rearrange("e s q i -> q (e s) i")
+        ro3 = w3_scales[0:E].rearrange("e s q i -> q (e s) i")
+        nc.sync.dma_start(offsets[:], offs)
+        nc.sync.dma_start(out=xw[:].bitcast(I32), in_=x_words[0].rearrange("p t r -> p (t r)").bitcast(I32))
+        load_scale_rows(nc.scalar, xs, x_scales[0], range(3))
+        load_scale_rows(nc.sync, w1s_sh, w1_scales[SHARED, 0], range(2))
+        nc.sync.dma_start(out=w1w_sh.bitcast(I32), in_=w1_words[SHARED, 0].bitcast(I32))
+        nc.sync.dma_start(out=w3w_sh.bitcast(I32), in_=w3_words[SHARED, 0].bitcast(I32))
+        load_scale_rows(nc.scalar, w1s_sh, w1_scales[SHARED, 0], range(2, 4))
+        load_scale_rows(nc.sync, w3s_sh, w3_scales[SHARED, 0], range(2))
+        load_scale_rows(nc.scalar, w3s_sh, w3_scales[SHARED, 0], range(2, 4))
+        load_scale_rows(nc.sync, xs, x_scales[0], range(3, 4))
+        load_scale_rows(nc.sync, w1s_ro, ro1)
+        load_scale_rows(nc.sync, w3s_ro, ro3)
+        load_scale_rows(nc.gpsimd, w2s, w2_scales.rearrange("e s q n -> q (e s) n"))
+        load_words(w1w_ro[0], w1_words[0:2])
+        load_words(w3w_ro[0], w3_words[0:2])
+        load_words(w2w, w2_words)
+        load_words(w1w_ro[1], w1_words[2:4])
+        load_words(w3w_ro[1], w3_words[2:4])
+
+        for j in range(T // GATHER):
+            cols = offsets[:, j * GATHER // 16 : (j + 1) * GATHER // 16]
+            nc.vector.tensor_copy(gw[j][:], xw[:].indirect(cols))
+        for j in range(T // GATHER):
+            cols = offsets[:, j * GATHER // 16 : (j + 1) * GATHER // 16]
+            nc.vector.tensor_copy(gs[j][:], xs[:].indirect(cols))
+
+        def first_layer(i, s):
+            e, b = steps[i]
+            if e == SHARED:
+                tok_w = xw[:, b * C : (b + 1) * C]
+                tok_s = xs[:, b * C : (b + 1) * C]
+                s1, s3 = w1s_sh, w3s_sh
+            else:
+                j, o = divmod(b * C, GATHER)
+                tok_w = gw[j][:, o : o + C]
+                tok_s = gs[j][:, o : o + C]
+                s1, s3 = w1s_ro[:, e * H : (e + 1) * H], w3s_ro[:, e * H : (e + 1) * H]
+            h = h_all[i]
+            u = S * i + s
+            a = a_banks[u % len(a_banks)]
+            b3 = b_banks[u % len(b_banks)]
+            for acc, words, scales in ((a, w1w[e], s1), (b3, w3w[e], s3)):
+                nc.tensor.matmul_mx(
+                    out=acc[:],
+                    lhsT=tok_w.bitcast(FP8X4),
+                    lhsT_scale=tok_s,
+                    rhs=words[:, 2 * PASS * s : 2 * PASS * (s + 1)].bitcast(FP4X4),
+                    rhs_scale=scales[:, PASS * s : PASS * (s + 1)],
+                    start=True,
+                    stop=True,
+                )
+            g = gate_sb if u == 0 else g_ring[u % len(g_ring)]
+            nc.scalar.activation(
+                out=g[:].rearrange("t (u p e) -> t u p e", u=2, e=2),
+                in_=a[:].rearrange("t (p u e) -> t u p e", u=2, e=2),
+                func=GELU,
+            )
+            nc.vector.tensor_tensor(
+                out=h[:, PASS * s : PASS * (s + 1)].rearrange("t (u p e) -> t u p e", u=2, e=2),
+                in0=b3[:].rearrange("t (p u e) -> t u p e", u=2, e=2),
+                in1=g[:].rearrange("t (u p e) -> t u p e", u=2, e=2),
+                op=MULT,
+            )
+            if u == 0:
+                nc.sync.dma_start(out=gate_sb[:], in_=gate)
+
+        def turn(i, s0, s1, xt):
+            words = h_all[i][:].bitcast(F32)
+            m = s1 - s0
+            for k in range(2 * m):
+                nc.tensor.transpose(
+                    xt[:, k * C : (k + 1) * C], words[:, (2 * s0 + k) * P : (2 * s0 + k + 1) * P], ident[:]
+                )
+            ht = ht_all[i][:, 4 * C * s0 : 4 * C * s1]
+            nc.scalar.copy(
+                out=ht.bitcast(F32).rearrange("p (s t u) -> p s t u", s=m, u=2),
+                in_=xt[:, : 2 * m * C].rearrange("p (s u t) -> p s t u", s=m, u=2),
+            )
+            nc.vector.quantize_mx(
+                out=hq_all[i][:, C * s0 : C * s1].bitcast(FP8X4),
+                scales=hs_all[i][:, C * s0 : C * s1],
+                in_=ht,
+            )
+
+        def second_layer(i):
+            e, b = steps[i]
+            hq, hs = hq_all[i], hs_all[i]
+            place = b if e == SHARED else 3
+            y = y_bank[:, place * C : (place + 1) * C]
+            for s in range(S):
+                m = e * S + s
+                nc.tensor.matmul_mx(
+                    out=y,
+                    lhsT=w2w[:, 2 * N * m : 2 * N * (m + 1)].bitcast(FP4X4),
+                    lhsT_scale=w2s[:, N * m : N * (m + 1)],
+                    rhs=hq[:, C * s : C * (s + 1)].bitcast(FP8X4),
+                    rhs_scale=hs[:, C * s : C * (s + 1)],
+                    start=(s == 0),
+                    stop=(s == S - 1),
+                )
+            if e != SHARED:
+                y_sb = y_all[e]
+                nc.scalar.copy(out=y_sb[:], in_=y)
+                nc.vector.tensor_tensor(
+                    out=routed[:].indirect(offsets[:, e * C // 16 : (e + 1) * C // 16]),
+                    in0=y_sb[:],
+                    in1=gate_sb[:, e * C : (e + 1) * C],
+                    op=MULT,
+                )
+            elif b == 2:
+                nc.vector.tensor_tensor(out=early[:], in0=y_bank[:, : 3 * C], in1=routed[:, : 3 * C], op=ADD)
+                nc.sync.dma_start(out=out[:, : 3 * C], in_=early[:])
+            elif b == 3:
+                nc.vector.tensor_tensor(out=last[:], in0=y, in1=routed[:, 3 * C :], op=ADD)
+                nc.sync.dma_start(out=out[:, 3 * C :], in_=last[:])
+
+        for i in range(n):
+            first_layer(i, 0)
+            if i >= 2:
+                second_layer(i - 2)
+            first_layer(i, 1)
+            if i >= 1:
+                turn(i - 1, 0, S, a_banks[S * i % len(a_banks)])
+        turn(n - 1, 0, 1, a_banks[0])
+        second_layer(n - 2)
+        turn(n - 1, 1, 2, a_banks[1])
+        second_layer(n - 1)

@@ -28,10 +28,7 @@ GATHER = 256
 def load_scale_rows(queue, plane, rows, which=range(4)):
     by_r = rows.rearrange("(q r) w -> r q w" if rows.ndim == 2 else "(q r) m w -> r q m w", r=4)
     for r in which:
-        place = plane[r:P:32, :].bitcast(I32)
-        if rows.ndim == 3:
-            place = place.rearrange("q (m w) -> q m w", m=rows.shape[1])
-        queue.dma_start(out=place, in_=by_r[r].bitcast(I32))
+        queue.dma_start(out=plane[r:P:32].bitcast(I32), in_=by_r[r].bitcast(I32))
 
 
 def tile_moe_shr_glu_gelu_kernel(
@@ -51,22 +48,15 @@ def tile_moe_shr_glu_gelu_kernel(
         offsets = keep.tile([P, T // 16], U16, name="offsets")
         xw = keep.tile([P, T], U32, name="xw", align_bytes=64)
         xs = keep.tile([P, T], U8, name="xs", align_bytes=64)
-        w1_sh = keep.tile([P, 3 * H], U8, name="w1_sh", align_bytes=64)
-        w3_sh = keep.tile([P, 3 * H], U8, name="w3_sh", align_bytes=64)
-        w1s_sh, w1w_sh = w1_sh[:, :H], w1_sh[:, H:]
-        w3s_sh, w3w_sh = w3_sh[:, :H], w3_sh[:, H:]
-        w1_ro = keep.tile([P, 3 * E * H], U8, name="w1_ro", align_bytes=64)
-        w3_ro = keep.tile([P, 3 * E * H], U8, name="w3_ro", align_bytes=64)
-        w1s_ro = w1_ro[:, E * H : 2 * E * H]
-        w3s_ro = w3_ro[:, E * H : 2 * E * H]
-        w1w_ro = (w1_ro[:, : E * H], w1_ro[:, 2 * E * H :])
-        w3w_ro = (w3_ro[:, : E * H], w3_ro[:, 2 * E * H :])
         w2_cols = (E + 1) * S * N
+        w1_sh = keep.tile([P, 3 * H], U8, name="w1_sh", align_bytes=64)
+        w1_ro = keep.tile([P, E, 3 * H], U8, name="w1_ro", align_bytes=64)
+        w3_sb = keep.tile([P, E + 1, 3 * H], U8, name="w3_sb", align_bytes=64)
         w2_sb = keep.tile([P, 3 * w2_cols], U8, name="w2_sb", align_bytes=64)
-        w2w = w2_sb[:, : 2 * w2_cols]
-        w2s = w2_sb[:, 2 * w2_cols :]
-        w1w = [w1w_ro[e // 2][:, 2 * H * (e % 2) : 2 * H * (e % 2 + 1)] for e in range(E)] + [w1w_sh]
-        w3w = [w3w_ro[e // 2][:, 2 * H * (e % 2) : 2 * H * (e % 2 + 1)] for e in range(E)] + [w3w_sh]
+        w1s = [w1_ro[:, e, :H] for e in range(E)] + [w1_sh[:, :H]]
+        w1w = [w1_ro[:, e, H:] for e in range(E)] + [w1_sh[:, H:]]
+        w3w = [w3_sb[:, e, H:] for e in range(E + 1)]
+        w2s, w2w = w2_sb[:, :w2_cols], w2_sb[:, w2_cols:]
         gate_sb = keep.tile([P, E * C], F32, name="gate_sb")
         ident = keep.tile([P, P], F32, name="ident")
         routed = keep.tile([P, T], F32, name="routed")
@@ -87,40 +77,39 @@ def tile_moe_shr_glu_gelu_kernel(
         for plane in (
             xs[:],
             w1_sh[:, : H + 32],
-            w3_sh[:, : H + 32],
-            w1_ro[:, E * H - 32 : 2 * E * H + 32],
-            w3_ro[:, E * H - 32 : 2 * E * H + 32],
-            w2_sb[:, 2 * w2_cols - 32 :],
+            w3_sb[:, :, : H + 32],
+            w1_ro[:, :, : H + 32],
+            w2_sb[:, : w2_cols + 32],
         ):
             nc.vector.memset(plane.bitcast(I32), 0)
         make_identity(nc, ident[:])
 
         def load_words(tile, words):
             nc.sync.dma_start(
-                out=tile.bitcast(I32).rearrange("p (m w) -> p m w", m=words.shape[0] * words.shape[1]),
+                out=tile.bitcast(I32),
                 in_=words.rearrange("e s p n -> p (e s) n").bitcast(I32),
             )
 
-        ro1 = w1_scales[0:E].rearrange("e s q i -> q (e s) i")
-        ro3 = w3_scales[0:E].rearrange("e s q i -> q (e s) i")
+        w3_rows = w3_scales.rearrange("e s q i -> q (e s) i")
         nc.sync.dma_start(offsets[:], offs)
         nc.sync.dma_start(out=xw[:].bitcast(I32), in_=x_words[0].rearrange("p t r -> p (t r)").bitcast(I32))
-        load_scale_rows(nc.scalar, xs, x_scales[0], range(3))
-        load_scale_rows(nc.sync, w1s_sh, w1_scales[SHARED, 0], range(2))
-        nc.sync.dma_start(out=w1w_sh.bitcast(I32), in_=w1_words[SHARED, 0].bitcast(I32))
-        nc.sync.dma_start(out=w3w_sh.bitcast(I32), in_=w3_words[SHARED, 0].bitcast(I32))
-        load_scale_rows(nc.scalar, w1s_sh, w1_scales[SHARED, 0], range(2, 4))
-        load_scale_rows(nc.sync, w3s_sh, w3_scales[SHARED, 0], range(2))
-        load_scale_rows(nc.scalar, w3s_sh, w3_scales[SHARED, 0], range(2, 4))
-        load_scale_rows(nc.sync, xs, x_scales[0], range(3, 4))
-        load_scale_rows(nc.sync, w1s_ro, ro1)
-        load_scale_rows(nc.sync, w3s_ro, ro3)
-        load_scale_rows(nc.gpsimd, w2s, w2_scales.rearrange("e s q n -> q (e s) n"))
-        load_words(w1w_ro[0], w1_words[0:2])
-        load_words(w3w_ro[0], w3_words[0:2])
-        load_words(w2w, w2_words)
-        load_words(w1w_ro[1], w1_words[2:4])
-        load_words(w3w_ro[1], w3_words[2:4])
+        load_scale_rows(nc.scalar, xs[:], x_scales[0], range(3))
+        nc.sync.dma_start(out=w1w[SHARED].bitcast(I32), in_=w1_words[SHARED, 0].bitcast(I32))
+        load_scale_rows(nc.sync, w1s[SHARED], w1_scales[SHARED, 0], range(2))
+        load_scale_rows(nc.scalar, w1s[SHARED], w1_scales[SHARED, 0], range(2, 4))
+        nc.sync.dma_start(out=w3w[SHARED].bitcast(I32), in_=w3_words[SHARED, 0].bitcast(I32))
+        load_scale_rows(nc.sync, w3_sb[:, :, :H], w3_rows, range(2))
+        load_scale_rows(nc.scalar, w3_sb[:, :, :H], w3_rows, range(2, 4))
+        load_scale_rows(nc.sync, xs[:], x_scales[0], range(3, 4))
+        load_scale_rows(nc.sync, w1_ro[:, :, :H], w1_scales[0:E].rearrange("e s q i -> q (e s) i"))
+        for e in range(2):
+            nc.sync.dma_start(out=w1w[e].bitcast(I32), in_=w1_words[e, 0].bitcast(I32))
+            nc.sync.dma_start(out=w3w[e].bitcast(I32), in_=w3_words[e, 0].bitcast(I32))
+        load_words(w1_ro[:, 2:4, H:], w1_words[2:4])
+        load_words(w3_sb[:, 2:4, H:], w3_words[2:4])
+        load_scale_rows(nc.sync, w2s.rearrange("p (m n) -> p m n", n=N), w2_scales.rearrange("e s q n -> q (e s) n"))
+        load_words(w2w.rearrange("p (m c) -> p m c", c=2 * N), w2_words)
+
 
         for j in range(T // GATHER):
             cols = offsets[:, j * GATHER // 16 : (j + 1) * GATHER // 16]
@@ -134,12 +123,11 @@ def tile_moe_shr_glu_gelu_kernel(
             if e == SHARED:
                 tok_w = xw[:, b * C : (b + 1) * C]
                 tok_s = xs[:, b * C : (b + 1) * C]
-                s1, s3 = w1s_sh, w3s_sh
             else:
                 j, o = divmod(b * C, GATHER)
                 tok_w = gw[j][:, o : o + C]
                 tok_s = gs[j][:, o : o + C]
-                s1, s3 = w1s_ro[:, e * H : (e + 1) * H], w3s_ro[:, e * H : (e + 1) * H]
+            s1, s3 = w1s[e], w3_sb[:, e, :H]
             h = h_all[i]
             u = S * i + s
             a = a_banks[u % len(a_banks)]
@@ -191,7 +179,7 @@ def tile_moe_shr_glu_gelu_kernel(
             e, b = steps[i]
             hq, hs = hq_all[i], hs_all[i]
             place = b if e == SHARED else 3
-            y = y_bank[:, place * C : (place + 1) * C]
+            y = y_bank[:, place * C : (place + 1) * C] if i < n - 1 else b_banks[S * n % len(b_banks)][:, :C]
             for s in range(S):
                 m = e * S + s
                 nc.tensor.matmul_mx(
@@ -221,12 +209,14 @@ def tile_moe_shr_glu_gelu_kernel(
 
         for i in range(n):
             first_layer(i, 0)
-            if i >= 2:
-                second_layer(i - 2)
+            if i >= 3:
+                second_layer(i - 3)
             first_layer(i, 1)
-            if i >= 1:
-                turn(i - 1, 0, S, a_banks[S * i % len(a_banks)])
+            if i >= 2:
+                turn(i - 2, 0, S, a_banks[S * i % len(a_banks)])
+        second_layer(n - 3)
+        turn(n - 2, 0, S, a_banks[1])
         turn(n - 1, 0, 1, a_banks[0])
+        turn(n - 1, 1, 2, a_banks[3])
         second_layer(n - 2)
-        turn(n - 1, 1, 2, a_banks[1])
         second_layer(n - 1)

@@ -51,11 +51,13 @@ def tile_moe_shr_glu_gelu_kernel(
         w2_cols = (E + 1) * S * N
         w1_sh = keep.tile([P, 3 * H], U8, name="w1_sh", align_bytes=64)
         w1_ro = keep.tile([P, E, 3 * H], U8, name="w1_ro", align_bytes=64)
-        w3_sb = keep.tile([P, E + 1, 3 * H], U8, name="w3_sb", align_bytes=64)
+        w3_sh = keep.tile([P, 3 * H], U8, name="w3_sh", align_bytes=64)
+        w3_ro = keep.tile([P, E, 3 * H], U8, name="w3_ro", align_bytes=64)
         w2_sb = keep.tile([P, 3 * w2_cols], U8, name="w2_sb", align_bytes=64)
         w1s = [w1_ro[:, e, :H] for e in range(E)] + [w1_sh[:, :H]]
         w1w = [w1_ro[:, e, H:] for e in range(E)] + [w1_sh[:, H:]]
-        w3w = [w3_sb[:, e, H:] for e in range(E + 1)]
+        w3s = [w3_ro[:, e, :H] for e in range(E)] + [w3_sh[:, :H]]
+        w3w = [w3_ro[:, e, H:] for e in range(E)] + [w3_sh[:, H:]]
         w2s, w2w = w2_sb[:, :w2_cols], w2_sb[:, w2_cols:]
         gate_sb = keep.tile([P, E * C], F32, name="gate_sb")
         ident = keep.tile([P, P], F32, name="ident")
@@ -77,8 +79,9 @@ def tile_moe_shr_glu_gelu_kernel(
         for plane in (
             xs[:],
             w1_sh[:, : H + 32],
-            w3_sb[:, :, : H + 32],
+            w3_sh[:, : H + 32],
             w1_ro[:, :, : H + 32],
+            w3_ro[:, :, : H + 32],
             w2_sb[:, : w2_cols + 32],
         ):
             nc.vector.memset(plane.bitcast(I32), 0)
@@ -90,23 +93,23 @@ def tile_moe_shr_glu_gelu_kernel(
                 in_=words.rearrange("e s p n -> p (e s) n").bitcast(I32),
             )
 
-        w3_rows = w3_scales.rearrange("e s q i -> q (e s) i")
+        def load_expert(e):
+            nc.sync.dma_start(out=w1w[e].bitcast(I32), in_=w1_words[e, 0].bitcast(I32))
+            nc.sync.dma_start(out=w3w[e].bitcast(I32), in_=w3_words[e, 0].bitcast(I32))
+
         nc.sync.dma_start(offsets[:], offs)
         nc.sync.dma_start(out=xw[:].bitcast(I32), in_=x_words[0].rearrange("p t r -> p (t r)").bitcast(I32))
         load_scale_rows(nc.scalar, xs[:], x_scales[0], range(3))
-        nc.sync.dma_start(out=w1w[SHARED].bitcast(I32), in_=w1_words[SHARED, 0].bitcast(I32))
         load_scale_rows(nc.sync, w1s[SHARED], w1_scales[SHARED, 0], range(2))
+        load_expert(SHARED)
         load_scale_rows(nc.scalar, w1s[SHARED], w1_scales[SHARED, 0], range(2, 4))
-        nc.sync.dma_start(out=w3w[SHARED].bitcast(I32), in_=w3_words[SHARED, 0].bitcast(I32))
-        load_scale_rows(nc.sync, w3_sb[:, :, :H], w3_rows, range(2))
-        load_scale_rows(nc.scalar, w3_sb[:, :, :H], w3_rows, range(2, 4))
+        load_scale_rows(nc.sync, w3s[SHARED], w3_scales[SHARED, 0], range(2))
+        load_scale_rows(nc.scalar, w3s[SHARED], w3_scales[SHARED, 0], range(2, 4))
         load_scale_rows(nc.sync, xs[:], x_scales[0], range(3, 4))
         load_scale_rows(nc.sync, w1_ro[:, :, :H], w1_scales[0:E].rearrange("e s q i -> q (e s) i"))
-        for e in range(2):
-            nc.sync.dma_start(out=w1w[e].bitcast(I32), in_=w1_words[e, 0].bitcast(I32))
-            nc.sync.dma_start(out=w3w[e].bitcast(I32), in_=w3_words[e, 0].bitcast(I32))
-        load_words(w1_ro[:, 2:4, H:], w1_words[2:4])
-        load_words(w3_sb[:, 2:4, H:], w3_words[2:4])
+        load_scale_rows(nc.sync, w3_ro[:, :, :H], w3_scales[0:E].rearrange("e s q i -> q (e s) i"))
+        for e in range(E):
+            load_expert(e)
         load_scale_rows(nc.sync, w2s.rearrange("p (m n) -> p m n", n=N), w2_scales.rearrange("e s q n -> q (e s) n"))
         load_words(w2w.rearrange("p (m c) -> p m c", c=2 * N), w2_words)
 
@@ -127,7 +130,7 @@ def tile_moe_shr_glu_gelu_kernel(
                 j, o = divmod(b * C, GATHER)
                 tok_w = gw[j][:, o : o + C]
                 tok_s = gs[j][:, o : o + C]
-            s1, s3 = w1s[e], w3_sb[:, e, :H]
+            s1, s3 = w1s[e], w3s[e]
             h = h_all[i]
             u = S * i + s
             a = a_banks[u % len(a_banks)]

@@ -78,11 +78,11 @@ def tile_moe_shr_glu_gelu_kernel(
 
         for plane in (
             xs[:],
-            w1_sh[:, : H + 32],
-            w3_sh[:, : H + 32],
-            w1_ro[:, :, : H + 32],
-            w3_ro[:, :, : H + 32],
-            w2_sb[:, : w2_cols + 32],
+            w1_sh[:, : H],
+            w3_sh[:, : H],
+            w1_ro[:, :, : H],
+            w3_ro[:, :, : H],
+            w2_sb[:, : w2_cols],
         ):
             nc.vector.memset(plane.bitcast(I32), 0)
         make_identity(nc, ident[:])
@@ -103,8 +103,8 @@ def tile_moe_shr_glu_gelu_kernel(
         load_scale_rows(nc.sync, w1s[SHARED], w1_scales[SHARED, 0], range(2))
         load_expert(SHARED)
         load_scale_rows(nc.scalar, w1s[SHARED], w1_scales[SHARED, 0], range(2, 4))
-        load_scale_rows(nc.sync, w3s[SHARED], w3_scales[SHARED, 0], range(2))
-        load_scale_rows(nc.scalar, w3s[SHARED], w3_scales[SHARED, 0], range(2, 4))
+        load_scale_rows(nc.sync, w3s[SHARED], w3_scales[SHARED, 0], (0, 1, 3))
+        load_scale_rows(nc.scalar, w3s[SHARED], w3_scales[SHARED, 0], (2,))
         load_scale_rows(nc.sync, xs[:], x_scales[0], range(3, 4))
         load_scale_rows(nc.sync, w1_ro[:, :, :H], w1_scales[0:E].rearrange("e s q i -> q (e s) i"))
         load_scale_rows(nc.sync, w3_ro[:, :, :H], w3_scales[0:E].rearrange("e s q i -> q (e s) i"))

from contextlib import ExitStack

import concourse.mybir as mybir
from concourse.masks import make_identity

K, T, E, C, H, N = 512, 512, 4, 128, 1024, 128
FLOPS = 2 * (E * C + T) * (2 * K * H + H * N)

F32 = mybir.dt.float32
BF16 = mybir.dt.bfloat16
I32 = mybir.dt.int32
U32 = mybir.dt.uint32
U16 = mybir.dt.uint16
U8 = mybir.dt.uint8
FP8X4 = mybir.dt.float8_e4m3fn_x4
FP4X4 = mybir.dt.float4_e2m1fn_x4
GELU = mybir.ActivationFunctionType.Gelu_apprx_tanh
MULT = mybir.AluOpType.mult
ADD = mybir.AluOpType.add

P = 128
PASS = 512
S = H // PASS
SHARED = E
GATHER = 256


def load_scale_rows(queue, plane, rows, which=range(4)):
    by_r = rows.rearrange("(q r) w -> r q w" if rows.ndim == 2 else "(q r) m w -> r q m w", r=4)
    for r in which:
        queue.dma_start(out=plane[r:P:32].bitcast(I32), in_=by_r[r].bitcast(I32))


def tile_moe_shr_glu_gelu_kernel(
    tc, x_words, x_scales, w1_words, w1_scales, w3_words, w3_scales, w2_words, w2_scales, gate, offs, out
):
    nc = tc.nc
    with ExitStack() as ctx:
        keep = ctx.enter_context(tc.tile_pool(name="keep", bufs=1))
        psum = ctx.enter_context(tc.psum_pool(name="psum", bufs=1))

        def tiles(name, count, shape, dtype):
            return [keep.tile(shape, dtype, name=f"{name}{j}", align_bytes=64) for j in range(count)]

        steps = [(SHARED, 0), (SHARED, 1)] + [(e, e) for e in range(E)] + [(SHARED, 2), (SHARED, 3)]
        n = len(steps)

        offsets = keep.tile([P, T // 16], U16, name="offsets")
        xw = keep.tile([P, T], U32, name="xw", align_bytes=64)
        xs = keep.tile([P, T], U8, name="xs", align_bytes=64)
        w2_cols = (E + 1) * S * N
        w1_sh = keep.tile([P, 3 * H], U8, name="w1_sh", align_bytes=64)
        w1_ro = keep.tile([P, E, 3 * H], U8, name="w1_ro", align_bytes=64)
        w3_sh = keep.tile([P, 3 * H], U8, name="w3_sh", align_bytes=64)
        w3_ro = keep.tile([P, E, 3 * H], U8, name="w3_ro", align_bytes=64)
        w2_sb = keep.tile([P, 3 * w2_cols], U8, name="w2_sb", align_bytes=64)
        w1s = [w1_ro[:, e, :H] for e in range(E)] + [w1_sh[:, :H]]
        w1w = [w1_ro[:, e, H:] for e in range(E)] + [w1_sh[:, H:]]
        w3s = [w3_ro[:, e, :H] for e in range(E)] + [w3_sh[:, :H]]
        w3w = [w3_ro[:, e, H:] for e in range(E)] + [w3_sh[:, H:]]
        w2s, w2w = w2_sb[:, :w2_cols], w2_sb[:, w2_cols:]
        gate_sb = keep.tile([P, E * C], F32, name="gate_sb")
        ident = keep.tile([P, P], F32, name="ident")
        routed = keep.tile([P, T], F32, name="routed")
        gw = tiles("gw", T // GATHER, [P, GATHER], U32)
        gs = tiles("gs", T // GATHER, [P, GATHER], U8)
        g_ring = tiles("g", 4, [P, PASS], F32)
        h_all = tiles("h", n, [P, H], BF16)
        ht_all = tiles("ht", n, [P, S * C * 4], BF16)
        hq_all = tiles("hq", n, [P, S * C], U32)
        hs_all = tiles("hs", n, [P, S * C], U8)
        y_all = tiles("y", E, [P, C], F32)
        early = keep.tile([P, 3 * C], F32, name="early")
        last = keep.tile([P, C], F32, name="last")
        a_banks = [psum.tile([P, PASS], F32, name=f"a_bank{j}") for j in range(4)]
        b_banks = [psum.tile([P, PASS], F32, name=f"b_bank{j}") for j in range(3)]
        y_bank = psum.tile([P, T], F32, name="y_bank")

        for plane in (
            xs[:],
            w1_sh[:, : H],
            w3_sh[:, : H],
            w1_ro[:, :, : H],
            w3_ro[:, :, : H],
            w2_sb[:, : w2_cols],
        ):
            nc.vector.memset(plane.bitcast(I32), 0)
        make_identity(nc, ident[:])

        def load_words(tile, words):
            nc.sync.dma_start(
                out=tile.bitcast(I32),
                in_=words.rearrange("e s p n -> p (e s) n").bitcast(I32),
            )

        def load_expert(e):
            nc.sync.dma_start(out=w1w[e].bitcast(I32), in_=w1_words[e, 0].bitcast(I32))
            nc.sync.dma_start(out=w3w[e].bitcast(I32), in_=w3_words[e, 0].bitcast(I32))

        nc.sync.dma_start(offsets[:], offs)
        nc.sync.dma_start(out=xw[:].bitcast(I32), in_=x_words[0].rearrange("p t r -> p (t r)").bitcast(I32))
        load_scale_rows(nc.scalar, xs[:], x_scales[0], range(3))
        load_scale_rows(nc.sync, w1s[SHARED], w1_scales[SHARED, 0], range(2))
        load_expert(SHARED)
        load_scale_rows(nc.scalar, w1s[SHARED], w1_scales[SHARED, 0], range(2, 4))
        load_scale_rows(nc.sync, w3s[SHARED], w3_scales[SHARED, 0], (0, 1, 3))
        load_scale_rows(nc.scalar, w3s[SHARED], w3_scales[SHARED, 0], (2,))
        load_scale_rows(nc.sync, xs[:], x_scales[0], range(3, 4))
        load_scale_rows(nc.sync, w1_ro[:, :, :H], w1_scales[0:E].rearrange("e s q i -> q (e s) i"))
        load_scale_rows(nc.sync, w3_ro[:, :, :H], w3_scales[0:E].rearrange("e s q i -> q (e s) i"))
        for e in range(E):
            load_expert(e)
        load_scale_rows(nc.sync, w2s.rearrange("p (m n) -> p m n", n=N), w2_scales.rearrange("e s q n -> q (e s) n"))
        load_words(w2w.rearrange("p (m c) -> p m c", c=2 * N), w2_words)


        for j in range(T // GATHER):
            cols = offsets[:, j * GATHER // 16 : (j + 1) * GATHER // 16]
            nc.vector.tensor_copy(gw[j][:], xw[:].indirect(cols))
        for j in range(T // GATHER):
            cols = offsets[:, j * GATHER // 16 : (j + 1) * GATHER // 16]
            nc.vector.tensor_copy(gs[j][:], xs[:].indirect(cols))

        def first_layer(i, s):
            e, b = steps[i]
            if e == SHARED:
                tok_w = xw[:, b * C : (b + 1) * C]
                tok_s = xs[:, b * C : (b + 1) * C]
            else:
                j, o = divmod(b * C, GATHER)
                tok_w = gw[j][:, o : o + C]
                tok_s = gs[j][:, o : o + C]
            s1, s3 = w1s[e], w3s[e]
            h = h_all[i]
            u = S * i + s
            a = a_banks[u % len(a_banks)]
            b3 = b_banks[u % len(b_banks)]
            for acc, words, scales in ((a, w1w[e], s1), (b3, w3w[e], s3)):
                nc.tensor.matmul_mx(
                    out=acc[:],
                    lhsT=tok_w.bitcast(FP8X4),
                    lhsT_scale=tok_s,
                    rhs=words[:, 2 * PASS * s : 2 * PASS * (s + 1)].bitcast(FP4X4),
                    rhs_scale=scales[:, PASS * s : PASS * (s + 1)],
                    start=True,
                    stop=True,
                )
            g = gate_sb if u == 0 else g_ring[u % len(g_ring)]
            nc.scalar.activation(
                out=g[:].rearrange("t (u p e) -> t u p e", u=2, e=2),
                in_=a[:].rearrange("t (p u e) -> t u p e", u=2, e=2),
                func=GELU,
            )
            nc.vector.tensor_tensor(
                out=h[:, PASS * s : PASS * (s + 1)].rearrange("t (u p e) -> t u p e", u=2, e=2),
                in0=b3[:].rearrange("t (p u e) -> t u p e", u=2, e=2),
                in1=g[:].rearrange("t (u p e) -> t u p e", u=2, e=2),
                op=MULT,
            )
            if u == 0:
                nc.sync.dma_start(out=gate_sb[:], in_=gate)

        def turn(i, s0, s1, xt):
            words = h_all[i][:].bitcast(F32)
            m = s1 - s0
            for k in range(2 * m):
                nc.tensor.transpose(
                    xt[:, k * C : (k + 1) * C], words[:, (2 * s0 + k) * P : (2 * s0 + k + 1) * P], ident[:]
                )
            ht = ht_all[i][:, 4 * C * s0 : 4 * C * s1]
            nc.scalar.copy(
                out=ht.bitcast(F32).rearrange("p (s t u) -> p s t u", s=m, u=2),
                in_=xt[:, : 2 * m * C].rearrange("p (s u t) -> p s t u", s=m, u=2),
            )
            nc.vector.quantize_mx(
                out=hq_all[i][:, C * s0 : C * s1].bitcast(FP8X4),
                scales=hs_all[i][:, C * s0 : C * s1],
                in_=ht,
            )

        def second_layer(i):
            e, b = steps[i]
            hq, hs = hq_all[i], hs_all[i]
            place = b if e == SHARED else 3
            y = y_bank[:, place * C : (place + 1) * C] if i < n - 1 else b_banks[S * n % len(b_banks)][:, :C]
            for s in range(S):
                m = e * S + s
                nc.tensor.matmul_mx(
                    out=y,
                    lhsT=w2w[:, 2 * N * m : 2 * N * (m + 1)].bitcast(FP4X4),
                    lhsT_scale=w2s[:, N * m : N * (m + 1)],
                    rhs=hq[:, C * s : C * (s + 1)].bitcast(FP8X4),
                    rhs_scale=hs[:, C * s : C * (s + 1)],
                    start=(s == 0),
                    stop=(s == S - 1),
                )
            if e != SHARED:
                y_sb = y_all[e]
                nc.scalar.copy(out=y_sb[:], in_=y)
                nc.vector.tensor_tensor(
                    out=routed[:].indirect(offsets[:, e * C // 16 : (e + 1) * C // 16]),
                    in0=y_sb[:],
                    in1=gate_sb[:, e * C : (e + 1) * C],
                    op=MULT,
                )
            elif b == 2:
                nc.vector.tensor_tensor(out=early[:], in0=y_bank[:, : 3 * C], in1=routed[:, : 3 * C], op=ADD)
                nc.sync.dma_start(out=out[:, : 3 * C], in_=early[:])
            elif b == 3:
                nc.vector.tensor_tensor(out=last[:], in0=y, in1=routed[:, 3 * C :], op=ADD)
                nc.sync.dma_start(out=out[:, 3 * C :], in_=last[:])

        for i in range(n):
            first_layer(i, 0)
            if i >= 3:
                second_layer(i - 3)
            first_layer(i, 1)
            if i >= 2:
                turn(i - 2, 0, S, a_banks[S * i % len(a_banks)])
        second_layer(n - 3)
        turn(n - 2, 0, S, a_banks[1])
        turn(n - 1, 0, 1, a_banks[0])
        turn(n - 1, 1, 2, a_banks[3])
        second_layer(n - 2)
        second_layer(n - 1)
